import numpy as np
import ml_dtypes

BF16 = ml_dtypes.bfloat16


def bf(x):
    return np.asarray(x, np.float32).astype(BF16)


def f32(x):
    return np.asarray(x, np.float32)


def f64(x):
    return np.asarray(x).astype(np.float64)


def striped(idx):
    return np.tile(idx.reshape(-1, 16).T, (8, 1))


S, K, M, N = 4096, 128, 128, 1024


def setup_inputs():
    return {"table": bf(np.random.standard_normal((K, S))), "w": bf(np.random.standard_normal((K, M)) / np.sqrt(K)), "offs": striped(np.random.permutation(np.tile(np.arange(S), 2))[:N])}


def reference(table, w, offs):
    idx = offs[:16].T.reshape(-1)
    x = f64(table)[:, idx]
    y = f64(w).T @ x
    return y

@@ -1,0 +1,43 @@
+import concourse.mybir as mybir
+
+BF16, F32, U16 = mybir.dt.bfloat16, mybir.dt.float32, mybir.dt.uint16
+
+P = 128
+WORDS = 4096
+TOKENS = 1024
+PIECE = 512
+PER_COLUMN = 16
+
+FLOPS = 2 * P * P * TOKENS
+
+
+def tile_gather_matmul_kernel(tc, table, w, offs, out):
+    nc = tc.nc
+    with (
+        tc.tile_pool(name="held", bufs=1) as held,
+        tc.psum_pool(name="psum", bufs=1) as psum,
+    ):
+        offsets = held.tile([P, TOKENS // PER_COLUMN], U16, name="offsets")
+        weights = held.tile([P, P], BF16, name="weights")
+        window = held.tile([P, WORDS], BF16, name="window")
+
+        half = WORDS // 2
+        nc.sync.dma_start(offsets[:], offs)
+        nc.scalar.dma_start(window[:, :half], table[:, :half])
+        nc.sync.dma_start(window[:, half:], table[:, half:])
+        nc.gpsimd.dma_start(weights[:], w)
+
+        for piece in range(TOKENS // PIECE):
+            columns = slice(piece * PIECE, (piece + 1) * PIECE)
+            entries = slice(piece * PIECE // PER_COLUMN, (piece + 1) * PIECE // PER_COLUMN)
+            bank = psum.tile([P, PIECE], F32, name=f"bank{piece}")
+            staged = held.tile([P, PIECE], F32, name=f"staged{piece}")
+            nc.tensor.matmul(
+                bank[:], weights[:], window[:].indirect(offsets[:, entries]), start=True, stop=True
+            )
+            if piece % 2 == 0:
+                nc.vector.tensor_copy(staged[:], bank[:])
+                nc.sync.dma_start(out[:, columns], staged[:])
+            else:
+                nc.scalar.copy(staged[:], bank[:])
+                nc.scalar.dma_start(out[:, columns], staged[:])

@@ -5,8 +5,10 @@ BF16, F32, U16 = mybir.dt.bfloat16, mybir.dt.float32, mybir.dt.uint16
 P = 128
 WORDS = 4096
 TOKENS = 1024
-PIECE = 512
+PIECE = 256
+BANK = 512
 PER_COLUMN = 16
+WARM_UPS = 6
 
 FLOPS = 2 * P * P * TOKENS
 
@@ -26,6 +28,12 @@ def tile_gather_matmul_kernel(tc, table, w, offs, out):
         nc.scalar.dma_start(window[:, :half], table[:, :half])
         nc.sync.dma_start(window[:, half:], table[:, half:])
         nc.gpsimd.dma_start(weights[:], w)
+
+        zeros = held.tile([P, BANK], BF16, name="zeros")
+        unread = psum.tile([P, BANK], F32, name="unread")
+        nc.vector.memset(zeros[:], 0.0)
+        for turn in range(WARM_UPS):
+            nc.tensor.matmul(unread[:], zeros[:, :P], zeros[:], start=True, stop=True)
 
         for piece in range(TOKENS // PIECE):
             columns = slice(piece * PIECE, (piece + 1) * PIECE)

@@ -6,9 +6,7 @@ P = 128
 WORDS = 4096
 TOKENS = 1024
 PIECE = 256
-BANK = 512
 PER_COLUMN = 16
-WARM_UPS = 6
 
 FLOPS = 2 * P * P * TOKENS
 
@@ -28,12 +26,6 @@ def tile_gather_matmul_kernel(tc, table, w, offs, out):
         nc.scalar.dma_start(window[:, :half], table[:, :half])
         nc.sync.dma_start(window[:, half:], table[:, half:])
         nc.gpsimd.dma_start(weights[:], w)
-
-        zeros = held.tile([P, BANK], BF16, name="zeros")
-        unread = psum.tile([P, BANK], F32, name="unread")
-        nc.vector.memset(zeros[:], 0.0)
-        for turn in range(WARM_UPS):
-            nc.tensor.matmul(unread[:], zeros[:, :P], zeros[:], start=True, stop=True)
 
         for piece in range(TOKENS // PIECE):
             columns = slice(piece * PIECE, (piece + 1) * PIECE)

@@ -23,9 +23,9 @@ def tile_gather_matmul_kernel(tc, table, w, offs, out):
 
         half = WORDS // 2
         nc.sync.dma_start(offsets[:], offs)
-        nc.scalar.dma_start(window[:, :half], table[:, :half])
-        nc.sync.dma_start(window[:, half:], table[:, half:])
-        nc.gpsimd.dma_start(weights[:], w)
+        nc.scalar.dma_start(weights[:], w)
+        nc.sync.dma_start(window[:, :half], table[:, :half])
+        nc.scalar.dma_start(window[:, half:], table[:, half:])
 
         for piece in range(TOKENS // PIECE):
             columns = slice(piece * PIECE, (piece + 1) * PIECE)
@@ -35,9 +35,6 @@ def tile_gather_matmul_kernel(tc, table, w, offs, out):
             nc.tensor.matmul(
                 bank[:], weights[:], window[:].indirect(offsets[:, entries]), start=True, stop=True
             )
-            if piece % 2 == 0:
-                nc.vector.tensor_copy(staged[:], bank[:])
-                nc.sync.dma_start(out[:, columns], staged[:])
-            else:
-                nc.scalar.copy(staged[:], bank[:])
-                nc.scalar.dma_start(out[:, columns], staged[:])
+            nc.vector.tensor_copy(staged[:], bank[:])
+            queue = nc.sync if piece % 2 == 0 else nc.scalar
+            queue.dma_start(out[:, columns], staged[:])

@@ -21,11 +21,9 @@ def tile_gather_matmul_kernel(tc, table, w, offs, out):
         weights = held.tile([P, P], BF16, name="weights")
         window = held.tile([P, WORDS], BF16, name="window")
 
-        half = WORDS // 2
+        nc.scalar.dma_start(window[:], table)
         nc.sync.dma_start(offsets[:], offs)
-        nc.scalar.dma_start(weights[:], w)
-        nc.sync.dma_start(window[:, :half], table[:, :half])
-        nc.scalar.dma_start(window[:, half:], table[:, half:])
+        nc.sync.dma_start(weights[:], w)
 
         for piece in range(TOKENS // PIECE):
             columns = slice(piece * PIECE, (piece + 1) * PIECE)

@@ -21,9 +21,9 @@ def tile_gather_matmul_kernel(tc, table, w, offs, out):
         weights = held.tile([P, P], BF16, name="weights")
         window = held.tile([P, WORDS], BF16, name="window")
 
-        nc.scalar.dma_start(window[:], table)
+        nc.sync.dma_start(window[:], table)
         nc.sync.dma_start(offsets[:], offs)
-        nc.sync.dma_start(weights[:], w)
+        nc.scalar.dma_start(weights[:], w)
 
         for piece in range(TOKENS // PIECE):
             columns = slice(piece * PIECE, (piece + 1) * PIECE)

@@ -34,5 +34,4 @@ def tile_gather_matmul_kernel(tc, table, w, offs, out):
                 bank[:], weights[:], window[:].indirect(offsets[:, entries]), start=True, stop=True
             )
             nc.vector.tensor_copy(staged[:], bank[:])
-            queue = nc.sync if piece % 2 == 0 else nc.scalar
-            queue.dma_start(out[:, columns], staged[:])
+            nc.sync.dma_start(out[:, columns], staged[:])

@@ -5,7 +5,8 @@ BF16, F32, U16 = mybir.dt.bfloat16, mybir.dt.float32, mybir.dt.uint16
 P = 128
 WORDS = 4096
 TOKENS = 1024
-PIECE = 256
+PIECE = 128
+PAIR = 2 * PIECE
 PER_COLUMN = 16
 
 FLOPS = 2 * P * P * TOKENS
@@ -25,13 +26,17 @@ def tile_gather_matmul_kernel(tc, table, w, offs, out):
         nc.sync.dma_start(offsets[:], offs)
         nc.scalar.dma_start(weights[:], w)
 
-        for piece in range(TOKENS // PIECE):
-            columns = slice(piece * PIECE, (piece + 1) * PIECE)
-            entries = slice(piece * PIECE // PER_COLUMN, (piece + 1) * PIECE // PER_COLUMN)
-            bank = psum.tile([P, PIECE], F32, name=f"bank{piece}")
-            staged = held.tile([P, PIECE], F32, name=f"staged{piece}")
-            nc.tensor.matmul(
-                bank[:], weights[:], window[:].indirect(offsets[:, entries]), start=True, stop=True
-            )
-            nc.vector.tensor_copy(staged[:], bank[:])
-            nc.sync.dma_start(out[:, columns], staged[:])
+        for pair in range(TOKENS // PAIR):
+            staged = held.tile([P, PAIR], F32, name=f"staged{pair}")
+            for half in range(2):
+                piece = 2 * pair + half
+                entries = slice(piece * PIECE // PER_COLUMN, (piece + 1) * PIECE // PER_COLUMN)
+                bank = psum.tile([P, PIECE], F32, name=f"bank{piece}")
+                nc.tensor.matmul(
+                    bank[:], weights[:], window[:].indirect(offsets[:, entries]), start=True, stop=True
+                )
+                if half == 0:
+                    nc.vector.tensor_copy(staged[:, 0:PIECE], bank[:])
+                else:
+                    nc.scalar.copy(staged[:, PIECE:PAIR], bank[:])
+            nc.sync.dma_start(out[:, pair * PAIR : (pair + 1) * PAIR], staged[:])

@@ -22,9 +22,9 @@ def tile_gather_matmul_kernel(tc, table, w, offs, out):
         weights = held.tile([P, P], BF16, name="weights")
         window = held.tile([P, WORDS], BF16, name="window")
 
-        nc.sync.dma_start(window[:], table)
+        nc.scalar.dma_start(window[:], table)
         nc.sync.dma_start(offsets[:], offs)
-        nc.scalar.dma_start(weights[:], w)
+        nc.sync.dma_start(weights[:], w)
 
         for pair in range(TOKENS // PAIR):
             staged = held.tile([P, PAIR], F32, name=f"staged{pair}")

import concourse.mybir as mybir

BF16, F32, U16 = mybir.dt.bfloat16, mybir.dt.float32, mybir.dt.uint16

P = 128
WORDS = 4096
TOKENS = 1024
PIECE = 128
PAIR = 2 * PIECE
PER_COLUMN = 16

FLOPS = 2 * P * P * TOKENS


def tile_gather_matmul_kernel(tc, table, w, offs, out):
    nc = tc.nc
    with (
        tc.tile_pool(name="held", bufs=1) as held,
        tc.psum_pool(name="psum", bufs=1) as psum,
    ):
        offsets = held.tile([P, TOKENS // PER_COLUMN], U16, name="offsets")
        weights = held.tile([P, P], BF16, name="weights")
        window = held.tile([P, WORDS], BF16, name="window")

        nc.scalar.dma_start(window[:], table)
        nc.sync.dma_start(offsets[:], offs)
        nc.sync.dma_start(weights[:], w)

        for pair in range(TOKENS // PAIR):
            staged = held.tile([P, PAIR], F32, name=f"staged{pair}")
            for half in range(2):
                piece = 2 * pair + half
                entries = slice(piece * PIECE // PER_COLUMN, (piece + 1) * PIECE // PER_COLUMN)
                bank = psum.tile([P, PIECE], F32, name=f"bank{piece}")
                nc.tensor.matmul(
                    bank[:], weights[:], window[:].indirect(offsets[:, entries]), start=True, stop=True
                )
                if half == 0:
                    nc.vector.tensor_copy(staged[:, 0:PIECE], bank[:])
                else:
                    nc.scalar.copy(staged[:, PIECE:PAIR], bank[:])
            nc.sync.dma_start(out[:, pair * PAIR : (pair + 1) * PAIR], staged[:])
